import numpy as np
import ml_dtypes


def mxq(x, axis, fmt="e4m3"):
    dtype, down = {"e4m3": (ml_dtypes.float8_e4m3fn, 7), "e5m2": (ml_dtypes.float8_e5m2, 14)}[fmt]
    v = np.moveaxis(np.asarray(x, np.float32).astype(ml_dtypes.bfloat16).astype(np.float64), axis, -1)
    blocks = v.reshape(v.shape[:-1] + (-1, 32))
    amax = np.abs(blocks).max(-1, keepdims=True)
    byte = np.maximum(np.where(amax > 0, np.frexp(amax)[1] - 1 + 127, 0) - down, 1)
    scale = np.exp2(byte - 127.0)
    codes = (blocks / scale).astype(np.float32).astype(dtype).astype(np.float64)
    return np.moveaxis((codes * scale).reshape(v.shape), -1, axis)


WIDE = False


def mx_kscale(k):
    if not WIDE:
        return np.ones(k)
    levels = np.array([10, -10, 5, -5, 0])
    if k % 512:
        return np.exp2(np.random.permutation(np.resize(levels, k // 32))).repeat(32)
    a = np.empty((k // 512, 16))
    for p in range(k // 512):
        a[p, :8] = np.random.permutation(np.resize(levels, 8))
        for g in range(8):
            far = levels[np.abs(levels - a[p, g]) >= 10]
            a[p, g + 8] = far[np.random.randint(len(far))]
    return np.exp2(a.ravel()).repeat(32)


def f64(x):
    return np.asarray(x).astype(np.float64)


def striped(idx):
    return np.tile(np.asarray(idx).reshape(-1, 16).T, (8, 1)).astype(np.uint16)


def unstriped(offs):
    return offs[:16].T.reshape(-1).astype(np.int64)


G, K, T, D, M = 128, 64, 2048, 512, 128


def setup_inputs():
    n = np.random.standard_normal
    s = mx_kscale(D)[:, None]
    grid = lambda x: np.round(x * 32) / 32
    x = grid(n((D, T))) * s
    idx = np.random.randint(0, T, (G, K))
    return {
        "xT": x.astype(np.float32),
        "w": (n((D, M)) / np.sqrt(D * K) / s).astype(np.float32),
        "bias": (0.3 * n((M, 1))).astype(np.float32),
        "offs": striped(idx.reshape(-1)),
    }


def reference(xT, w, bias, offs):
    x = f64(xT)[:, unstriped(offs)]
    y = mxq(f64(w), 0, "e4m3").T @ mxq(x.reshape(D, G, K).sum(-1), 0, "e4m3")
    y = y + f64(bias)
    return y

@@ -1,0 +1,160 @@
+from contextlib import ExitStack
+
+import concourse.mybir as mybir
+from concourse.masks import make_identity
+
+G, K, T, D, M = 128, 64, 2048, 512, 128
+FLOPS = 2 * D * M * G
+
+F32 = mybir.dt.float32
+BF16 = mybir.dt.bfloat16
+U32 = mybir.dt.uint32
+U16 = mybir.dt.uint16
+U8 = mybir.dt.uint8
+FP8X4 = mybir.dt.float8_e4m3fn_x4
+IDENT = mybir.ActivationFunctionType.Identity
+ADD = mybir.AluOpType.add
+MULT = mybir.AluOpType.mult
+X = mybir.AxisListType.X
+
+P = 128
+PACK = 4
+STEP = 16
+CHUNKS = ((32, 32, 32, 32), (32, 32, 32, 16, 16))
+GP_T = 0
+
+
+def tile_attend_bag_bias_kernel(tc, xT, w, bias, offs, out):
+    nc = tc.nc
+    with ExitStack() as ctx:
+        hold = ctx.enter_context(tc.tile_pool(name="hold", bufs=1))
+        gots = ctx.enter_context(tc.tile_pool(name="gots", bufs=4))
+        ring = ctx.enter_context(tc.tile_pool(name="ring", bufs=3))
+        psum_a = ctx.enter_context(tc.psum_pool(name="psum_a", bufs=3))
+        psum_b = ctx.enter_context(tc.psum_pool(name="psum_b", bufs=3))
+        psum = ctx.enter_context(tc.psum_pool(name="psum", bufs=1))
+
+        lists = hold.tile([P, G * K // 16], U16, name="lists")
+        nc.sync.dma_start(lists[:], offs)
+
+        ident = hold.tile([P, P], F32, name="ident")
+        make_identity(nc, ident[:])
+
+        x_rows = xT.rearrange("(p j) c -> p j c", j=PACK)
+        windows = []
+        casts = []
+        for pair, widths in ((0, (512, 512, 512, 512)), (1, (512, 512, 512, 512))):
+            window = hold.tile([P, T * 2], BF16, name=f"window{pair}")
+            pairs = window[:].rearrange("p (c e) -> p c e", e=2)
+            c0 = 0
+            for k, width in enumerate(widths):
+                raw = hold.tile([P, 2, width], F32, name=f"raw{pair}_{k}")
+                nc.sync.dma_start(raw[:], x_rows[:, 2 * pair : 2 * pair + 2, c0 : c0 + width])
+                casts.append((pairs[:, c0 : c0 + width, :], raw[:].rearrange("p e c -> p c e")))
+                c0 += width
+            windows.append(window)
+
+        w_raw = hold.tile([P, PACK, M], F32, name="w_raw")
+        nc.sync.dma_start(w_raw[:], w.rearrange("(p j) m -> p j m", j=PACK))
+        bias_col = hold.tile([P, 1], F32, name="bias_col")
+        nc.sync.dma_start(bias_col[:], bias)
+
+        for dst, src in casts[:4]:
+            nc.vector.tensor_copy(dst, src)
+
+        e = hold.tile([P, G, PACK], F32, name="e")
+
+        def gather(pair, b0):
+            got = gots.tile([P, STEP * K * 2], BF16, name="got")
+            nc.vector.tensor_copy(
+                got[:].bitcast(U32),
+                windows[pair][:].bitcast(U32).indirect(lists[:, b0 * K // 16 : (b0 + STEP) * K // 16]),
+            )
+            return got
+
+        def widen(got, wide, s, nb):
+            q = P // nb
+            rows = got[:].rearrange("p (b t q e) -> p e t b q", t=K // q, q=q, e=2)
+            to = wide[:].rearrange("p (e t b q) -> p e t b q", e=2, t=K // q, q=q)
+            split = (K // q) * (16 - GP_T) // 16
+            for h in range(2):
+                nc.scalar.copy(to[:, h, :split, s : s + STEP, :], rows[:, h, :split])
+                if GP_T:
+                    nc.gpsimd.tensor_scalar(to[:, h, split:, s : s + STEP, :], rows[:, h, split:], 1.0, 0.0, MULT, ADD)
+
+        def turn(wide, nb):
+            q = P // nb
+            turned = psum_a.tile([P, 2, P], F32, name="turned")
+            for h in range(2):
+                for t in range(K // q):
+                    at = (h * (K // q) + t) * P
+                    nc.tensor.matmul(
+                        turned[:, h, :], wide[:, at : at + P], ident[:],
+                        is_transpose=True, start=(t == 0), stop=(t == K // q - 1),
+                    )
+            return turned
+
+        def turn_back(turned):
+            part = ring.tile([P, 2, P], F32, name="part")
+            nc.scalar.copy(part[:], turned[:])
+            back = psum_b.tile([P, 2, P], F32, name="back")
+            for h in range(2):
+                nc.tensor.transpose(back[:, h, :], part[:, h, :], ident[:])
+            return back
+
+        def reduce(back, pair, b0, nb):
+            nc.vector.tensor_reduce(
+                out=e[:, b0 : b0 + nb, 2 * pair : 2 * pair + 2].rearrange("p b h -> p h b"),
+                in_=back[:].rearrange("p h (b q) -> p h b q", q=P // nb),
+                axis=X,
+                op=ADD,
+            )
+
+        turned_q, back_q = [], []
+        for pair, sizes in enumerate(CHUNKS):
+            b0 = 0
+            for nb in sizes:
+                wide = ring.tile([P, 2 * nb * K], F32, name="wide")
+                for s in range(0, nb, STEP):
+                    widen(gather(pair, b0 + s), wide, s, nb)
+                if pair == 0 and b0 < 64:
+                    for dst, src in casts[4 + b0 // 16 : 6 + b0 // 16]:
+                        nc.scalar.copy(dst, src)
+                turned_q.append((turn(wide, nb), pair, b0, nb))
+                if len(turned_q) > 1:
+                    turned, *rest = turned_q.pop(0)
+                    back_q.append((turn_back(turned), *rest))
+                if len(back_q) > 1:
+                    reduce(*back_q.pop(0))
+                b0 += nb
+
+        w_bf = hold.tile([P, M * PACK], BF16, name="w_bf", align_bytes=64)
+        w_codes = hold.tile([P, M], U32, name="w_codes", align_bytes=64)
+        w_scales = hold.tile([P, M], U8, name="w_scales", align_bytes=64)
+        nc.vector.tensor_copy(w_bf[:].rearrange("p (m j) -> p m j", j=PACK), w_raw[:].rearrange("p j m -> p m j"))
+        nc.vector.quantize_mx(out=w_codes[:].bitcast(FP8X4), scales=w_scales[:], in_=w_bf[:])
+
+        for turned, *rest in turned_q:
+            back_q.append((turn_back(turned), *rest))
+        for item in back_q:
+            reduce(*item)
+
+        e_bf = hold.tile([P, G * PACK], BF16, name="e_bf", align_bytes=64)
+        e_codes = hold.tile([P, G], U32, name="e_codes", align_bytes=64)
+        e_scales = hold.tile([P, G], U8, name="e_scales", align_bytes=64)
+        nc.vector.tensor_copy(e_bf[:], e[:].rearrange("p g j -> p (g j)"))
+        nc.vector.quantize_mx(out=e_codes[:].bitcast(FP8X4), scales=e_scales[:], in_=e_bf[:])
+
+        acc = psum.tile([M, G], F32, name="acc")
+        nc.tensor.matmul_mx(
+            out=acc[:],
+            lhsT=w_codes[:].bitcast(FP8X4),
+            lhsT_scale=w_scales[:],
+            rhs=e_codes[:].bitcast(FP8X4),
+            rhs_scale=e_scales[:],
+            start=True,
+            stop=True,
+        )
+        y = hold.tile([M, G], F32, name="y")
+        nc.scalar.activation(y[:], acc[:], IDENT, bias=bias_col[:])
+        nc.sync.dma_start(out, y[:])

@@ -21,7 +21,7 @@ P = 128
 PACK = 4
 STEP = 16
 CHUNKS = ((32, 32, 32, 32), (32, 32, 32, 16, 16))
-GP_T = 0
+SHARES = ((12, 0, 4),) * 15 + ((8, 8, 0),)
 
 
 def tile_attend_bag_bias_kernel(tc, xT, w, bias, offs, out):
@@ -43,7 +43,7 @@ def tile_attend_bag_bias_kernel(tc, xT, w, bias, offs, out):
         x_rows = xT.rearrange("(p j) c -> p j c", j=PACK)
         windows = []
         casts = []
-        for pair, widths in ((0, (512, 512, 512, 512)), (1, (512, 512, 512, 512))):
+        for pair, widths in ((0, (512, 512, 512, 256, 256)), (1, (512, 512, 512, 512))):
             window = hold.tile([P, T * 2], BF16, name=f"window{pair}")
             pairs = window[:].rearrange("p (c e) -> p c e", e=2)
             c0 = 0
@@ -59,8 +59,11 @@ def tile_attend_bag_bias_kernel(tc, xT, w, bias, offs, out):
         bias_col = hold.tile([P, 1], F32, name="bias_col")
         nc.sync.dma_start(bias_col[:], bias)
 
-        for dst, src in casts[:4]:
-            nc.vector.tensor_copy(dst, src)
+        for k, (dst, src) in enumerate(casts[:5]):
+            if k in (1, 3):
+                nc.scalar.copy(dst, src)
+            else:
+                nc.vector.tensor_copy(dst, src)
 
         e = hold.tile([P, G, PACK], F32, name="e")
 
@@ -72,15 +75,20 @@ def tile_attend_bag_bias_kernel(tc, xT, w, bias, offs, out):
             )
             return got
 
-        def widen(got, wide, s, nb):
+        def widen(index, got, wide, s, nb):
             q = P // nb
             rows = got[:].rearrange("p (b t q e) -> p e t b q", t=K // q, q=q, e=2)
             to = wide[:].rearrange("p (e t b q) -> p e t b q", e=2, t=K // q, q=q)
-            split = (K // q) * (16 - GP_T) // 16
+            n_t = K // q
+            share = SHARES[index]
+            on_s = n_t * share[0] // 16
+            on_v = on_s + n_t * share[1] // 16
             for h in range(2):
-                nc.scalar.copy(to[:, h, :split, s : s + STEP, :], rows[:, h, :split])
-                if GP_T:
-                    nc.gpsimd.tensor_scalar(to[:, h, split:, s : s + STEP, :], rows[:, h, split:], 1.0, 0.0, MULT, ADD)
+                nc.scalar.copy(to[:, h, :on_s, s : s + STEP, :], rows[:, h, :on_s])
+                if on_v > on_s:
+                    nc.vector.tensor_copy(to[:, h, on_s:on_v, s : s + STEP, :], rows[:, h, on_s:on_v])
+                if n_t > on_v:
+                    nc.gpsimd.tensor_scalar(to[:, h, on_v:, s : s + STEP, :], rows[:, h, on_v:], 1.0, 0.0, MULT, ADD)
 
         def turn(wide, nb):
             q = P // nb
@@ -116,9 +124,9 @@ def tile_attend_bag_bias_kernel(tc, xT, w, bias, offs, out):
             for nb in sizes:
                 wide = ring.tile([P, 2 * nb * K], F32, name="wide")
                 for s in range(0, nb, STEP):
-                    widen(gather(pair, b0 + s), wide, s, nb)
+                    widen(pair * 8 + (b0 + s) // STEP, gather(pair, b0 + s), wide, s, nb)
                 if pair == 0 and b0 < 64:
-                    for dst, src in casts[4 + b0 // 16 : 6 + b0 // 16]:
+                    for dst, src in casts[5 + b0 // 16 : 7 + b0 // 16]:
                         nc.scalar.copy(dst, src)
                 turned_q.append((turn(wide, nb), pair, b0, nb))
                 if len(turned_q) > 1:

@@ -14,24 +14,24 @@ U8 = mybir.dt.uint8
 FP8X4 = mybir.dt.float8_e4m3fn_x4
 IDENT = mybir.ActivationFunctionType.Identity
 ADD = mybir.AluOpType.add
-MULT = mybir.AluOpType.mult
 X = mybir.AxisListType.X
 
 P = 128
 PACK = 4
 STEP = 16
-CHUNKS = ((32, 32, 32, 32), (32, 32, 32, 16, 16))
-SHARES = ((12, 0, 4),) * 15 + ((8, 8, 0),)
+CHUNKS = ((32, 32, 32, 32), (32, 32, 32, 16, 8, 8))
+CASTS = ((0, False), (0, False), (32, False), (64, False))
+LAG = 2
 
 
 def tile_attend_bag_bias_kernel(tc, xT, w, bias, offs, out):
     nc = tc.nc
     with ExitStack() as ctx:
         hold = ctx.enter_context(tc.tile_pool(name="hold", bufs=1))
-        gots = ctx.enter_context(tc.tile_pool(name="gots", bufs=4))
+        gots = ctx.enter_context(tc.tile_pool(name="gots", bufs=6))
         ring = ctx.enter_context(tc.tile_pool(name="ring", bufs=3))
         psum_a = ctx.enter_context(tc.psum_pool(name="psum_a", bufs=3))
-        psum_b = ctx.enter_context(tc.psum_pool(name="psum_b", bufs=3))
+        psum_b = ctx.enter_context(tc.psum_pool(name="psum_b", bufs=4))
         psum = ctx.enter_context(tc.psum_pool(name="psum", bufs=1))
 
         lists = hold.tile([P, G * K // 16], U16, name="lists")
@@ -46,6 +46,9 @@ def tile_attend_bag_bias_kernel(tc, xT, w, bias, offs, out):
         for pair, widths in ((0, (512, 512, 512, 256, 256)), (1, (512, 512, 512, 512))):
             window = hold.tile([P, T * 2], BF16, name=f"window{pair}")
             pairs = window[:].rearrange("p (c e) -> p c e", e=2)
+            if pair == 1:
+                w_raw = hold.tile([P, PACK, M], F32, name="w_raw")
+                nc.sync.dma_start(w_raw[:], w.rearrange("(p j) m -> p j m", j=PACK))
             c0 = 0
             for k, width in enumerate(widths):
                 raw = hold.tile([P, 2, width], F32, name=f"raw{pair}_{k}")
@@ -54,8 +57,6 @@ def tile_attend_bag_bias_kernel(tc, xT, w, bias, offs, out):
                 c0 += width
             windows.append(window)
 
-        w_raw = hold.tile([P, PACK, M], F32, name="w_raw")
-        nc.sync.dma_start(w_raw[:], w.rearrange("(p j) m -> p j m", j=PACK))
         bias_col = hold.tile([P, 1], F32, name="bias_col")
         nc.sync.dma_start(bias_col[:], bias)
 
@@ -65,40 +66,40 @@ def tile_attend_bag_bias_kernel(tc, xT, w, bias, offs, out):
             else:
                 nc.vector.tensor_copy(dst, src)
 
+        w_bf = hold.tile([P, M * PACK], BF16, name="w_bf", align_bytes=64)
+        w_codes = hold.tile([P, M], U32, name="w_codes", align_bytes=64)
+        w_scales = hold.tile([P, M], U8, name="w_scales", align_bytes=64)
+
         e = hold.tile([P, G, PACK], F32, name="e")
 
-        def gather(pair, b0):
+        def gather(pair, b0, nb=STEP):
             got = gots.tile([P, STEP * K * 2], BF16, name="got")
             nc.vector.tensor_copy(
-                got[:].bitcast(U32),
-                windows[pair][:].bitcast(U32).indirect(lists[:, b0 * K // 16 : (b0 + STEP) * K // 16]),
+                got[:, : nb * K * 2].bitcast(U32),
+                windows[pair][:].bitcast(U32).indirect(lists[:, b0 * K // 16 : (b0 + nb) * K // 16]),
             )
             return got
 
-        def widen(index, got, wide, s, nb):
+        def widen(got, wide, s, nb, at_end):
             q = P // nb
-            rows = got[:].rearrange("p (b t q e) -> p e t b q", t=K // q, q=q, e=2)
-            to = wide[:].rearrange("p (e t b q) -> p e t b q", e=2, t=K // q, q=q)
             n_t = K // q
-            share = SHARES[index]
-            on_s = n_t * share[0] // 16
-            on_v = on_s + n_t * share[1] // 16
-            for h in range(2):
-                nc.scalar.copy(to[:, h, :on_s, s : s + STEP, :], rows[:, h, :on_s])
-                if on_v > on_s:
-                    nc.vector.tensor_copy(to[:, h, on_s:on_v, s : s + STEP, :], rows[:, h, on_s:on_v])
-                if n_t > on_v:
-                    nc.gpsimd.tensor_scalar(to[:, h, on_v:, s : s + STEP, :], rows[:, h, on_v:], 1.0, 0.0, MULT, ADD)
+            step = min(nb, STEP)
+            rows = got[:, : step * K * 2].rearrange("p (b t q e) -> p e t b q", t=n_t, q=q, e=2)
+            to = wide[:].rearrange("p (t b q) -> p t b q", b=nb, q=q)
+            nc.scalar.copy(to[:, :n_t, s : s + step, :], rows[:, 0])
+            adder = nc.vector if at_end else nc.gpsimd
+            adder.tensor_tensor(
+                to[:, n_t:, s : s + step, :], rows[:, 1, : n_t // 2], rows[:, 1, n_t // 2 :], ADD
+            )
 
         def turn(wide, nb):
-            q = P // nb
+            n_t = nb // 2
             turned = psum_a.tile([P, 2, P], F32, name="turned")
-            for h in range(2):
-                for t in range(K // q):
-                    at = (h * (K // q) + t) * P
+            for h, (first, end) in enumerate(((0, n_t), (n_t, n_t * 3 // 2))):
+                for t in range(first, end):
                     nc.tensor.matmul(
-                        turned[:, h, :], wide[:, at : at + P], ident[:],
-                        is_transpose=True, start=(t == 0), stop=(t == K // q - 1),
+                        turned[:, h, :], wide[:, t * P : (t + 1) * P], ident[:],
+                        is_transpose=True, start=(t == first), stop=(t == end - 1),
                     )
             return turned
 
@@ -122,25 +123,26 @@ def tile_attend_bag_bias_kernel(tc, xT, w, bias, offs, out):
         for pair, sizes in enumerate(CHUNKS):
             b0 = 0
             for nb in sizes:
-                wide = ring.tile([P, 2 * nb * K], F32, name="wide")
-                for s in range(0, nb, STEP):
-                    widen(pair * 8 + (b0 + s) // STEP, gather(pair, b0 + s), wide, s, nb)
-                if pair == 0 and b0 < 64:
-                    for dst, src in casts[5 + b0 // 16 : 7 + b0 // 16]:
-                        nc.scalar.copy(dst, src)
+                wide = ring.tile([P, 2 * nb * K * 3 // 4], F32, name="wide")
+                step = min(nb, STEP)
+                for s in range(0, nb, step):
+                    widen(gather(pair, b0 + s, step), wide, s, nb, pair == 1 and b0 >= 112)
+                for (at, on_v), (dst, src) in zip(CASTS, casts[5:]):
+                    if (pair, b0) == (0, at):
+                        if on_v:
+                            nc.vector.tensor_copy(dst, src)
+                        else:
+                            nc.scalar.copy(dst, src)
+                if pair == 0 and b0 == 0:
+                    nc.scalar.copy(w_bf[:].rearrange("p (m j) -> p m j", j=PACK), w_raw[:].rearrange("p j m -> p m j"))
+                    nc.vector.quantize_mx(out=w_codes[:].bitcast(FP8X4), scales=w_scales[:], in_=w_bf[:])
                 turned_q.append((turn(wide, nb), pair, b0, nb))
                 if len(turned_q) > 1:
                     turned, *rest = turned_q.pop(0)
                     back_q.append((turn_back(turned), *rest))
-                if len(back_q) > 1:
+                if len(back_q) > LAG:
                     reduce(*back_q.pop(0))
                 b0 += nb
-
-        w_bf = hold.tile([P, M * PACK], BF16, name="w_bf", align_bytes=64)
-        w_codes = hold.tile([P, M], U32, name="w_codes", align_bytes=64)
-        w_scales = hold.tile([P, M], U8, name="w_scales", align_bytes=64)
-        nc.vector.tensor_copy(w_bf[:].rearrange("p (m j) -> p m j", j=PACK), w_raw[:].rearrange("p j m -> p m j"))
-        nc.vector.quantize_mx(out=w_codes[:].bitcast(FP8X4), scales=w_scales[:], in_=w_bf[:])
 
         for turned, *rest in turned_q:
             back_q.append((turn_back(turned), *rest))

@@ -19,8 +19,8 @@ X = mybir.AxisListType.X
 P = 128
 PACK = 4
 STEP = 16
-CHUNKS = ((32, 32, 32, 32), (32, 32, 32, 16, 8, 8))
-CASTS = ((0, False), (0, False), (32, False), (64, False))
+CHUNKS = ((64, 32, 32), (32, 32, 32, 16, 8, 8))
+CASTS = ((0, 0), (512, 0), (1024, 0), (1536, 64))
 LAG = 2
 
 
@@ -35,42 +35,41 @@ def tile_attend_bag_bias_kernel(tc, xT, w, bias, offs, out):
         psum = ctx.enter_context(tc.psum_pool(name="psum", bufs=1))
 
         lists = hold.tile([P, G * K // 16], U16, name="lists")
-        nc.sync.dma_start(lists[:], offs)
 
         ident = hold.tile([P, P], F32, name="ident")
         make_identity(nc, ident[:])
 
         x_rows = xT.rearrange("(p j) c -> p j c", j=PACK)
-        windows = []
-        casts = []
-        for pair, widths in ((0, (512, 512, 512, 256, 256)), (1, (512, 512, 512, 512))):
-            window = hold.tile([P, T * 2], BF16, name=f"window{pair}")
-            pairs = window[:].rearrange("p (c e) -> p c e", e=2)
-            if pair == 1:
-                w_raw = hold.tile([P, PACK, M], F32, name="w_raw")
-                nc.sync.dma_start(w_raw[:], w.rearrange("(p j) m -> p j m", j=PACK))
-            c0 = 0
-            for k, width in enumerate(widths):
-                raw = hold.tile([P, 2, width], F32, name=f"raw{pair}_{k}")
-                nc.sync.dma_start(raw[:], x_rows[:, 2 * pair : 2 * pair + 2, c0 : c0 + width])
-                casts.append((pairs[:, c0 : c0 + width, :], raw[:].rearrange("p e c -> p c e")))
-                c0 += width
-            windows.append(window)
-
+        raws = [hold.tile([P, 2, T], F32, name=f"raw{pair}") for pair in range(2)]
+        windows = [hold.tile([P, T * 2], BF16, name=f"window{pair}") for pair in range(2)]
+        w_raw = hold.tile([P, PACK, M], F32, name="w_raw")
         bias_col = hold.tile([P, 1], F32, name="bias_col")
+        nc.sync.dma_start(lists[:], offs)
+        for c0 in range(0, T, 512):
+            nc.sync.dma_start(raws[0][:, :, c0 : c0 + 512], x_rows[:, :2, c0 : c0 + 512])
+        nc.sync.dma_start(w_raw[:], w.rearrange("(p j) m -> p j m", j=PACK))
+        for h in range(2):
+            nc.sync.dma_start(raws[1][:, h, :], x_rows[:, 2 + h, :])
         nc.sync.dma_start(bias_col[:], bias)
 
-        for k, (dst, src) in enumerate(casts[:5]):
-            if k in (1, 3):
-                nc.scalar.copy(dst, src)
-            else:
-                nc.vector.tensor_copy(dst, src)
+        def cast(copy, pair, c0, c1):
+            copy(
+                windows[pair][:, 2 * c0 : 2 * c1].rearrange("p (c e) -> p c e", e=2),
+                raws[pair][:, :, c0:c1].rearrange("p e c -> p c e"),
+            )
+
+        cast(nc.vector.tensor_copy, 0, 0, 512)
+        cast(nc.scalar.copy, 0, 512, 1024)
+        cast(nc.vector.tensor_copy, 0, 1024, 1536)
+        cast(nc.scalar.copy, 0, 1536, 1696)
+        cast(nc.vector.tensor_copy, 0, 1696, 2048)
 
         w_bf = hold.tile([P, M * PACK], BF16, name="w_bf", align_bytes=64)
         w_codes = hold.tile([P, M], U32, name="w_codes", align_bytes=64)
         w_scales = hold.tile([P, M], U8, name="w_scales", align_bytes=64)
 
-        e = hold.tile([P, G, PACK], F32, name="e")
+        e = hold.tile([P, PACK, G], F32, name="e")
+        e_bf = hold.tile([P, G, PACK], BF16, name="e_bf", align_bytes=64)
 
         def gather(pair, b0, nb=STEP):
             got = gots.tile([P, STEP * K * 2], BF16, name="got")
@@ -80,22 +79,25 @@ def tile_attend_bag_bias_kernel(tc, xT, w, bias, offs, out):
             )
             return got
 
-        def widen(got, wide, s, nb, at_end):
+        def widen(got, wide, s, nb, adder, added):
             q = P // nb
             n_t = K // q
             step = min(nb, STEP)
             rows = got[:, : step * K * 2].rearrange("p (b t q e) -> p e t b q", t=n_t, q=q, e=2)
             to = wide[:].rearrange("p (t b q) -> p t b q", b=nb, q=q)
-            nc.scalar.copy(to[:, :n_t, s : s + step, :], rows[:, 0])
-            adder = nc.vector if at_end else nc.gpsimd
-            adder.tensor_tensor(
-                to[:, n_t:, s : s + step, :], rows[:, 1, : n_t // 2], rows[:, 1, n_t // 2 :], ADD
-            )
+            if added == 1:
+                nc.scalar.copy(to[:, :n_t, s : s + step, :], rows[:, 0])
+            for h in range(2 - added, 2):
+                first = h * n_t if added == 1 else h * n_t // 2
+                adder.tensor_tensor(
+                    to[:, first : first + n_t // 2, s : s + step, :], rows[:, h, : n_t // 2], rows[:, h, n_t // 2 :], ADD
+                )
 
-        def turn(wide, nb):
+        def turn(wide, nb, added):
             n_t = nb // 2
+            mid = n_t if added == 1 else n_t // 2
             turned = psum_a.tile([P, 2, P], F32, name="turned")
-            for h, (first, end) in enumerate(((0, n_t), (n_t, n_t * 3 // 2))):
+            for h, (first, end) in enumerate(((0, mid), (mid, mid + n_t // 2))):
                 for t in range(first, end):
                     nc.tensor.matmul(
                         turned[:, h, :], wide[:, t * P : (t + 1) * P], ident[:],
@@ -111,12 +113,9 @@ def tile_attend_bag_bias_kernel(tc, xT, w, bias, offs, out):
                 nc.tensor.transpose(back[:, h, :], part[:, h, :], ident[:])
             return back
 
-        def reduce(back, pair, b0, nb):
+        def reduce(out_, back, nb):
             nc.vector.tensor_reduce(
-                out=e[:, b0 : b0 + nb, 2 * pair : 2 * pair + 2].rearrange("p b h -> p h b"),
-                in_=back[:].rearrange("p h (b q) -> p h b q", q=P // nb),
-                axis=X,
-                op=ADD,
+                out=out_, in_=back[:].rearrange("p h (b q) -> p h b q", q=P // nb), axis=X, op=ADD
             )
 
         turned_q, back_q = [], []
@@ -125,35 +124,37 @@ def tile_attend_bag_bias_kernel(tc, xT, w, bias, offs, out):
             for nb in sizes:
                 wide = ring.tile([P, 2 * nb * K * 3 // 4], F32, name="wide")
                 step = min(nb, STEP)
+                added = 2 if b0 + nb == G and pair == 1 else 1
                 for s in range(0, nb, step):
-                    widen(gather(pair, b0 + s, step), wide, s, nb, pair == 1 and b0 >= 112)
-                for (at, on_v), (dst, src) in zip(CASTS, casts[5:]):
+                    widen(gather(pair, b0 + s, step), wide, s, nb, nc.vector if nb == 8 else nc.gpsimd, added)
+                for c0, at in CASTS:
                     if (pair, b0) == (0, at):
-                        if on_v:
-                            nc.vector.tensor_copy(dst, src)
-                        else:
-                            nc.scalar.copy(dst, src)
+                        cast(nc.scalar.copy, 1, c0, c0 + 512)
                 if pair == 0 and b0 == 0:
                     nc.scalar.copy(w_bf[:].rearrange("p (m j) -> p m j", j=PACK), w_raw[:].rearrange("p j m -> p m j"))
-                    nc.vector.quantize_mx(out=w_codes[:].bitcast(FP8X4), scales=w_scales[:], in_=w_bf[:])
-                turned_q.append((turn(wide, nb), pair, b0, nb))
+                turned_q.append((turn(wide, nb, added), pair, b0, nb))
                 if len(turned_q) > 1:
                     turned, *rest = turned_q.pop(0)
                     back_q.append((turn_back(turned), *rest))
                 if len(back_q) > LAG:
-                    reduce(*back_q.pop(0))
+                    back, pr, b, n = back_q.pop(0)
+                    reduce(e[:, 2 * pr : 2 * pr + 2, b : b + n], back, n)
                 b0 += nb
 
         for turned, *rest in turned_q:
             back_q.append((turn_back(turned), *rest))
-        for item in back_q:
-            reduce(*item)
+        for back, pr, b, n in back_q[:-1]:
+            reduce(e[:, 2 * pr : 2 * pr + 2, b : b + n], back, n)
+        nc.vector.quantize_mx(out=w_codes[:].bitcast(FP8X4), scales=w_scales[:], in_=w_bf[:])
+        back, pr, b, n = back_q[-1]
+        nc.vector.tensor_copy(e_bf[:, :b, :], e[:, :, :b].rearrange("p j g -> p g j"))
+        nc.vector.tensor_copy(e_bf[:, b:, :2], e[:, :2, b:].rearrange("p j g -> p g j"))
+        with nc.allow_low_precision(reason="the sums are float32; only the result is rounded"):
+            reduce(e_bf[:, b:, 2:].rearrange("p g j -> p j g"), back, n)
 
-        e_bf = hold.tile([P, G * PACK], BF16, name="e_bf", align_bytes=64)
         e_codes = hold.tile([P, G], U32, name="e_codes", align_bytes=64)
         e_scales = hold.tile([P, G], U8, name="e_scales", align_bytes=64)
-        nc.vector.tensor_copy(e_bf[:], e[:].rearrange("p g j -> p (g j)"))
-        nc.vector.quantize_mx(out=e_codes[:].bitcast(FP8X4), scales=e_scales[:], in_=e_bf[:])
+        nc.vector.quantize_mx(out=e_codes[:].bitcast(FP8X4), scales=e_scales[:], in_=e_bf[:].rearrange("p g j -> p (g j)"))
 
         acc = psum.tile([M, G], F32, name="acc")
         nc.tensor.matmul_mx(

@@ -19,8 +19,8 @@ X = mybir.AxisListType.X
 P = 128
 PACK = 4
 STEP = 16
-CHUNKS = ((64, 32, 32), (32, 32, 32, 16, 8, 8))
-CASTS = ((0, 0), (512, 0), (1024, 0), (1536, 64))
+CHUNKS = ((64, 64), (32, 32, 32, 16, 8, 8))
+CASTS = ((0, 0), (512, 0), (1024, 0), (1536, 0))
 LAG = 2
 
 
@@ -45,8 +45,8 @@ def tile_attend_bag_bias_kernel(tc, xT, w, bias, offs, out):
         w_raw = hold.tile([P, PACK, M], F32, name="w_raw")
         bias_col = hold.tile([P, 1], F32, name="bias_col")
         nc.sync.dma_start(lists[:], offs)
-        for c0 in range(0, T, 512):
-            nc.sync.dma_start(raws[0][:, :, c0 : c0 + 512], x_rows[:, :2, c0 : c0 + 512])
+        for c0, c1 in ((0, 1024), (1024, 1536), (1536, 2048)):
+            nc.sync.dma_start(raws[0][:, :, c0:c1], x_rows[:, :2, c0:c1])
         nc.sync.dma_start(w_raw[:], w.rearrange("(p j) m -> p j m", j=PACK))
         for h in range(2):
             nc.sync.dma_start(raws[1][:, h, :], x_rows[:, 2 + h, :])
@@ -126,7 +126,7 @@ def tile_attend_bag_bias_kernel(tc, xT, w, bias, offs, out):
                 step = min(nb, STEP)
                 added = 2 if b0 + nb == G and pair == 1 else 1
                 for s in range(0, nb, step):
-                    widen(gather(pair, b0 + s, step), wide, s, nb, nc.vector if nb == 8 else nc.gpsimd, added)
+                    widen(gather(pair, b0 + s, step), wide, s, nb, nc.vector if added == 2 else nc.gpsimd, added)
                 for c0, at in CASTS:
                     if (pair, b0) == (0, at):
                         cast(nc.scalar.copy, 1, c0, c0 + 512)

from contextlib import ExitStack

import concourse.mybir as mybir
from concourse.masks import make_identity

G, K, T, D, M = 128, 64, 2048, 512, 128
FLOPS = 2 * D * M * G

F32 = mybir.dt.float32
BF16 = mybir.dt.bfloat16
U32 = mybir.dt.uint32
U16 = mybir.dt.uint16
U8 = mybir.dt.uint8
FP8X4 = mybir.dt.float8_e4m3fn_x4
IDENT = mybir.ActivationFunctionType.Identity
ADD = mybir.AluOpType.add
X = mybir.AxisListType.X

P = 128
PACK = 4
STEP = 16
CHUNKS = ((64, 64), (32, 32, 32, 16, 8, 8))
CASTS = ((0, 0), (512, 0), (1024, 0), (1536, 0))
LAG = 2


def tile_attend_bag_bias_kernel(tc, xT, w, bias, offs, out):
    nc = tc.nc
    with ExitStack() as ctx:
        hold = ctx.enter_context(tc.tile_pool(name="hold", bufs=1))
        gots = ctx.enter_context(tc.tile_pool(name="gots", bufs=6))
        ring = ctx.enter_context(tc.tile_pool(name="ring", bufs=3))
        psum_a = ctx.enter_context(tc.psum_pool(name="psum_a", bufs=3))
        psum_b = ctx.enter_context(tc.psum_pool(name="psum_b", bufs=4))
        psum = ctx.enter_context(tc.psum_pool(name="psum", bufs=1))

        lists = hold.tile([P, G * K // 16], U16, name="lists")

        ident = hold.tile([P, P], F32, name="ident")
        make_identity(nc, ident[:])

        x_rows = xT.rearrange("(p j) c -> p j c", j=PACK)
        raws = [hold.tile([P, 2, T], F32, name=f"raw{pair}") for pair in range(2)]
        windows = [hold.tile([P, T * 2], BF16, name=f"window{pair}") for pair in range(2)]
        w_raw = hold.tile([P, PACK, M], F32, name="w_raw")
        bias_col = hold.tile([P, 1], F32, name="bias_col")
        nc.sync.dma_start(lists[:], offs)
        for c0, c1 in ((0, 1024), (1024, 1536), (1536, 2048)):
            nc.sync.dma_start(raws[0][:, :, c0:c1], x_rows[:, :2, c0:c1])
        nc.sync.dma_start(w_raw[:], w.rearrange("(p j) m -> p j m", j=PACK))
        for h in range(2):
            nc.sync.dma_start(raws[1][:, h, :], x_rows[:, 2 + h, :])
        nc.sync.dma_start(bias_col[:], bias)

        def cast(copy, pair, c0, c1):
            copy(
                windows[pair][:, 2 * c0 : 2 * c1].rearrange("p (c e) -> p c e", e=2),
                raws[pair][:, :, c0:c1].rearrange("p e c -> p c e"),
            )

        cast(nc.vector.tensor_copy, 0, 0, 512)
        cast(nc.scalar.copy, 0, 512, 1024)
        cast(nc.vector.tensor_copy, 0, 1024, 1536)
        cast(nc.scalar.copy, 0, 1536, 1696)
        cast(nc.vector.tensor_copy, 0, 1696, 2048)

        w_bf = hold.tile([P, M * PACK], BF16, name="w_bf", align_bytes=64)
        w_codes = hold.tile([P, M], U32, name="w_codes", align_bytes=64)
        w_scales = hold.tile([P, M], U8, name="w_scales", align_bytes=64)

        e = hold.tile([P, PACK, G], F32, name="e")
        e_bf = hold.tile([P, G, PACK], BF16, name="e_bf", align_bytes=64)

        def gather(pair, b0, nb=STEP):
            got = gots.tile([P, STEP * K * 2], BF16, name="got")
            nc.vector.tensor_copy(
                got[:, : nb * K * 2].bitcast(U32),
                windows[pair][:].bitcast(U32).indirect(lists[:, b0 * K // 16 : (b0 + nb) * K // 16]),
            )
            return got

        def widen(got, wide, s, nb, adder, added):
            q = P // nb
            n_t = K // q
            step = min(nb, STEP)
            rows = got[:, : step * K * 2].rearrange("p (b t q e) -> p e t b q", t=n_t, q=q, e=2)
            to = wide[:].rearrange("p (t b q) -> p t b q", b=nb, q=q)
            if added == 1:
                nc.scalar.copy(to[:, :n_t, s : s + step, :], rows[:, 0])
            for h in range(2 - added, 2):
                first = h * n_t if added == 1 else h * n_t // 2
                adder.tensor_tensor(
                    to[:, first : first + n_t // 2, s : s + step, :], rows[:, h, : n_t // 2], rows[:, h, n_t // 2 :], ADD
                )

        def turn(wide, nb, added):
            n_t = nb // 2
            mid = n_t if added == 1 else n_t // 2
            turned = psum_a.tile([P, 2, P], F32, name="turned")
            for h, (first, end) in enumerate(((0, mid), (mid, mid + n_t // 2))):
                for t in range(first, end):
                    nc.tensor.matmul(
                        turned[:, h, :], wide[:, t * P : (t + 1) * P], ident[:],
                        is_transpose=True, start=(t == first), stop=(t == end - 1),
                    )
            return turned

        def turn_back(turned):
            part = ring.tile([P, 2, P], F32, name="part")
            nc.scalar.copy(part[:], turned[:])
            back = psum_b.tile([P, 2, P], F32, name="back")
            for h in range(2):
                nc.tensor.transpose(back[:, h, :], part[:, h, :], ident[:])
            return back

        def reduce(out_, back, nb):
            nc.vector.tensor_reduce(
                out=out_, in_=back[:].rearrange("p h (b q) -> p h b q", q=P // nb), axis=X, op=ADD
            )

        turned_q, back_q = [], []
        for pair, sizes in enumerate(CHUNKS):
            b0 = 0
            for nb in sizes:
                wide = ring.tile([P, 2 * nb * K * 3 // 4], F32, name="wide")
                step = min(nb, STEP)
                added = 2 if b0 + nb == G and pair == 1 else 1
                for s in range(0, nb, step):
                    widen(gather(pair, b0 + s, step), wide, s, nb, nc.vector if added == 2 else nc.gpsimd, added)
                for c0, at in CASTS:
                    if (pair, b0) == (0, at):
                        cast(nc.scalar.copy, 1, c0, c0 + 512)
                if pair == 0 and b0 == 0:
                    nc.scalar.copy(w_bf[:].rearrange("p (m j) -> p m j", j=PACK), w_raw[:].rearrange("p j m -> p m j"))
                turned_q.append((turn(wide, nb, added), pair, b0, nb))
                if len(turned_q) > 1:
                    turned, *rest = turned_q.pop(0)
                    back_q.append((turn_back(turned), *rest))
                if len(back_q) > LAG:
                    back, pr, b, n = back_q.pop(0)
                    reduce(e[:, 2 * pr : 2 * pr + 2, b : b + n], back, n)
                b0 += nb

        for turned, *rest in turned_q:
            back_q.append((turn_back(turned), *rest))
        for back, pr, b, n in back_q[:-1]:
            reduce(e[:, 2 * pr : 2 * pr + 2, b : b + n], back, n)
        nc.vector.quantize_mx(out=w_codes[:].bitcast(FP8X4), scales=w_scales[:], in_=w_bf[:])
        back, pr, b, n = back_q[-1]
        nc.vector.tensor_copy(e_bf[:, :b, :], e[:, :, :b].rearrange("p j g -> p g j"))
        nc.vector.tensor_copy(e_bf[:, b:, :2], e[:, :2, b:].rearrange("p j g -> p g j"))
        with nc.allow_low_precision(reason="the sums are float32; only the result is rounded"):
            reduce(e_bf[:, b:, 2:].rearrange("p g j -> p j g"), back, n)

        e_codes = hold.tile([P, G], U32, name="e_codes", align_bytes=64)
        e_scales = hold.tile([P, G], U8, name="e_scales", align_bytes=64)
        nc.vector.quantize_mx(out=e_codes[:].bitcast(FP8X4), scales=e_scales[:], in_=e_bf[:].rearrange("p g j -> p (g j)"))

        acc = psum.tile([M, G], F32, name="acc")
        nc.tensor.matmul_mx(
            out=acc[:],
            lhsT=w_codes[:].bitcast(FP8X4),
            lhsT_scale=w_scales[:],
            rhs=e_codes[:].bitcast(FP8X4),
            rhs_scale=e_scales[:],
            start=True,
            stop=True,
        )
        y = hold.tile([M, G], F32, name="y")
        nc.scalar.activation(y[:], acc[:], IDENT, bias=bias_col[:])
        nc.sync.dma_start(out, y[:])
